import numpy as np
import ml_dtypes


def mxq(x, axis, fmt="e4m3"):
    dtype, down = {"e4m3": (ml_dtypes.float8_e4m3fn, 7), "e5m2": (ml_dtypes.float8_e5m2, 14)}[fmt]
    v = np.moveaxis(np.asarray(x, np.float32).astype(ml_dtypes.bfloat16).astype(np.float64), axis, -1)
    blocks = v.reshape(v.shape[:-1] + (-1, 32))
    amax = np.abs(blocks).max(-1, keepdims=True)
    byte = np.maximum(np.where(amax > 0, np.frexp(amax)[1] - 1 + 127, 0) - down, 1)
    scale = np.exp2(byte - 127.0)
    codes = (blocks / scale).astype(np.float32).astype(dtype).astype(np.float64)
    return np.moveaxis((codes * scale).reshape(v.shape), -1, axis)


WIDE = False


def mx_kscale(k):
    if not WIDE:
        return np.ones(k)
    levels = np.array([10, -10, 5, -5, 0])
    if k % 512:
        return np.exp2(np.random.permutation(np.resize(levels, k // 32))).repeat(32)
    a = np.empty((k // 512, 16))
    for p in range(k // 512):
        a[p, :8] = np.random.permutation(np.resize(levels, 8))
        for g in range(8):
            far = levels[np.abs(levels - a[p, g]) >= 10]
            a[p, g + 8] = far[np.random.randint(len(far))]
    return np.exp2(a.ravel()).repeat(32)


def f64(x):
    return np.asarray(x).astype(np.float64)


def striped(idx):
    return np.tile(np.asarray(idx).reshape(-1, 16).T, (8, 1)).astype(np.uint16)


def unstriped(offs):
    return offs[:16].T.reshape(-1).astype(np.int64)


E2M1 = np.array([0.0, 0.5, 1.0, 1.5, 2.0, 3.0, 4.0, 6.0, -0.0, -0.5, -1.0, -1.5, -2.0, -3.0, -4.0, -6.0])


def pack_weight(w, fmt):
    k, n = w.shape
    w = f64(np.asarray(w, np.float32).astype(ml_dtypes.bfloat16)).reshape(k // 32, 32, n)
    amax = np.abs(w).max(1)
    if fmt == "e4m3":
        byte = np.frexp(amax)[1] - 1 + 127 - 7
    else:
        mant, ex = np.frexp(amax / 6.0)
        byte = np.where(mant > 0.5, ex, ex - 1) + 127
    byte = np.clip(np.where(amax > 0, byte, 1), 1, 254)
    scaled = (w * np.exp2(127.0 - byte)[:, None, :]).reshape(k, n).astype(np.float32)
    by_word = np.ascontiguousarray(scaled.reshape(k // 512, 128, 4, n).transpose(0, 1, 3, 2))
    if fmt == "e4m3":
        words = by_word.astype(ml_dtypes.float8_e4m3fn).view(np.uint8)
    else:
        c = by_word.astype(ml_dtypes.float4_e2m1fn).view(np.uint8) & 0xF
        words = (c[..., 0::2] | (c[..., 1::2] << 4)).reshape(k // 512, 128, 2 * n)
    return np.ascontiguousarray(words), np.ascontiguousarray(byte.astype(np.uint8).reshape(k // 512, 16, n))


def unpack_weight(words, scales, fmt):
    g, _, n = scales.shape
    words = np.ascontiguousarray(words).reshape(g, 128, n, -1)
    if fmt == "e4m3":
        vals = words.view(ml_dtypes.float8_e4m3fn).astype(np.float64)
    else:
        nib = np.empty((g, 128, n, 4), np.uint8)
        nib[..., 0::2] = words & 0xF
        nib[..., 1::2] = words >> 4
        vals = E2M1[nib]
    vals = vals * np.repeat(np.exp2(scales.astype(np.float64) - 127.0), 8, axis=1)[..., None]
    return vals.transpose(0, 1, 3, 2).reshape(g * 512, n)


def sigmoid(v):
    return 1.0 / (1.0 + np.exp(-v))


D, E, T, I, Q = 512, 512, 2048, 512, 128


def setup_inputs():
    n = np.random.standard_normal
    idx = np.random.permutation(T)[:I]
    fd = mx_kscale(D)
    fe = mx_kscale(E)
    fi = mx_kscale(I)
    ti = np.ones(T)
    ti[idx] = fi
    keysp = pack_weight(n((D, T)) / fd[:, None], "e2m1")
    valsp = pack_weight(n((E, T)) / fe[:, None], "e2m1")
    return {
        "query": (n((D, Q)) * 0.5 / np.sqrt(D) * fd[:, None]).astype(np.float32),
        "query2": (n((D, Q)) * 0.8 / np.sqrt(D) * fd[:, None]).astype(np.float32),
        "keys_words": keysp[0],
        "keys_scales": keysp[1],
        "gout": (n((E, Q)) * 1 / np.sqrt(E) * fe[:, None]).astype(np.float32),
        "vals_words": valsp[0],
        "vals_scales": valsp[1],
        "size": (np.random.uniform(0.5, 2.0, (1, I))).astype(np.float32),
        "fs": (np.random.uniform(128.0, 512.0, (1, I)) * fi).astype(np.float32),
        "keyrows": (n((D, T)) / ti).astype(np.float32),
        "res": (n((Q, D)) * 4.0).astype(np.float32),
        "offs": striped(idx),
    }


def reference(query, query2, keys_words, keys_scales, gout, vals_words, vals_scales, size, fs, keyrows, res, offs):
    idx = unstriped(offs)
    keysu = unpack_weight(keys_words, keys_scales, "e2m1")
    valsu = unpack_weight(vals_words, vals_scales, "e2m1")
    queryq = mxq(f64(query), 0, "e4m3")
    keysidxg = keysu[:, idx]
    a = queryq.T @ keysidxg
    query2q = mxq(f64(query2), 0, "e4m3")
    b = query2q.T @ keysidxg
    r = np.exp(a - np.max(a, axis=1, keepdims=True))
    gt = sigmoid(b)
    p = r * gt
    z = np.sum(p, axis=1, keepdims=True)
    goutq = mxq(f64(gout), 0, "e4m3")
    valsidxg = valsu[:, idx]
    c0 = goutq.T @ valsidxg
    dz = np.sum(c0 * p * f64(size) / np.square(z) * (-1.0), axis=1, keepdims=True)
    dp = c0 / z * f64(size) + dz
    dgt = dp * r
    db = dgt * gt * (1.0 - gt)
    gs = db * f64(fs)
    gt1 = gs.T
    kt = f64(keyrows)[:, idx].T
    gt1q = mxq(gt1, 0, "e4m3")
    ktq = mxq(kt, 0, "e4m3")
    gq = gt1q.T @ ktq
    y = gq + f64(res)
    return y

@@ -1,0 +1,173 @@
+from contextlib import ExitStack
+
+import concourse.mybir as mybir
+from concourse.masks import make_identity
+
+D, E, T, I, Q = 512, 512, 2048, 512, 128
+FLOPS = 2 * Q * I * (2 * D + E) + 2 * I * Q * D
+
+F32 = mybir.dt.float32
+BF16 = mybir.dt.bfloat16
+I32 = mybir.dt.int32
+U32 = mybir.dt.uint32
+U16 = mybir.dt.uint16
+U8 = mybir.dt.uint8
+FP8X4 = mybir.dt.float8_e4m3fn_x4
+FP4X4 = mybir.dt.float4_e2m1fn_x4
+ACT = mybir.ActivationFunctionType
+ALU = mybir.AluOpType
+AXIS = mybir.AxisListType
+
+P = 128
+PACK = 4
+
+
+def tile_attend_bgatedexp_b_q_kernel(tc, query, query2, keys_words, keys_scales, gout, vals_words, vals_scales,
+                                      size, fs, keyrows, res, offs, out):
+    nc = tc.nc
+    with ExitStack() as ctx:
+        keep = ctx.enter_context(tc.tile_pool(name="keep", bufs=1))
+        psum = ctx.enter_context(tc.psum_pool(name="psum", bufs=1))
+
+        offsets = keep.tile([P, I // 16], U16, name="offsets")
+        nc.sync.dma_start(offsets[:], offs)
+
+        warm = keep.tile([P, 1], F32, name="warm")
+        warm2 = keep.tile([P, 1], F32, name="warm2")
+        nc.gpsimd.memset(warm[:], 0.0)
+        nc.scalar.activation(warm2[:], warm[:], ACT.Sigmoid)
+
+        def load_words(words, name):
+            pool_words = keep.tile([P, T], U16, name=name, align_bytes=64)
+            nc.sync.dma_start(pool_words[:].bitcast(I32), words[0].bitcast(I32))
+            return pool_words
+
+        def load_scales(scales, name):
+            pool_scales = keep.tile([P, T], U8, name=name, align_bytes=64)
+            nc.vector.memset(pool_scales[:].bitcast(I32), 0)
+            for quad in range(4):
+                nc.sync.dma_start(pool_scales[32 * quad:32 * quad + 4, :].bitcast(I32),
+                                  scales[0, 4 * quad:4 * quad + 4, :].bitcast(I32))
+            return pool_scales
+
+        def load_rows(rows, name):
+            raw = keep.tile([P, PACK, Q], F32, name=name)
+            nc.sync.dma_start(raw[:], rows.rearrange("(p j) w -> p j w", j=PACK))
+            return raw
+
+        def load_slot(vec, name):
+            col = keep.tile([P, PACK], F32, name=name)
+            nc.sync.dma_start(col[:], vec.rearrange("o (p t) -> (o p) t", t=PACK))
+            return col
+
+        kw = load_words(keys_words, "kw")
+        ks = load_scales(keys_scales, "ks")
+        q2_raw = load_rows(query2, "q2_raw")
+        q_raw = load_rows(query, "q_raw")
+        vw = load_words(vals_words, "vw")
+        vs = load_scales(vals_scales, "vs")
+        g_raw = load_rows(gout, "g_raw")
+        size_col = load_slot(size, "size_col")
+        fs_col = load_slot(fs, "fs_col")
+        kr = []
+        for j in range(4):
+            rows = keep.tile([P, T], F32, name="kr%d" % j)
+            nc.sync.dma_start(rows[:], keyrows[j * P:(j + 1) * P, :])
+            kr.append(rows)
+        res_sb = keep.tile([P, D], F32, name="res_sb")
+        nc.sync.dma_start(res_sb[:], res)
+
+        ident = keep.tile([P, P], F32, name="ident")
+        make_identity(nc, ident[:])
+
+        def gather(window, dtype, name):
+            got = keep.tile([P, I], dtype, name=name, align_bytes=64)
+            nc.vector.tensor_copy(got[:], window[:].indirect(offsets[:]))
+            return got
+
+        def quantize(grouped, name):
+            codes = keep.tile([P, P], U32, name=name + "_codes", align_bytes=64)
+            scales = keep.tile([P, P], U8, name=name + "_scales", align_bytes=64)
+            nc.vector.quantize_mx(out=codes[:].bitcast(FP8X4), scales=scales[:], in_=grouped[:])
+            return codes, scales
+
+        def interleave(raw, name):
+            grouped = keep.tile([P, Q * PACK], BF16, name=name, align_bytes=64)
+            nc.scalar.copy(grouped[:].rearrange("p (c i t) -> p c t i", i=4, t=PACK),
+                           raw[:].rearrange("p t (c i) -> p c t i", i=4))
+            return grouped
+
+        def scores(lhs, words, scales, name):
+            acc = psum.tile([P, I], F32, name=name)
+            nc.tensor.matmul_mx(out=acc[:], lhsT=lhs[0][:].bitcast(FP8X4), lhsT_scale=lhs[1][:],
+                                rhs=words[:].bitcast(FP4X4), rhs_scale=scales[:], start=True, stop=True)
+            return acc
+
+        def spread(col, name):
+            acc = psum.tile([P, PACK, P], F32, name=name)
+            for t in range(PACK):
+                nc.tensor.transpose(acc[:, t, :], col[:, t:t + 1].to_broadcast([P, P]), ident[:])
+            return acc
+
+        def turn_and_quantize(rows_bf, name, tag):
+            words = rows_bf[:].bitcast(F32)
+            turned = psum.tile([P, 2, P], F32, name=name + "_ps", tag=tag)
+            for u in range(2):
+                nc.tensor.transpose(turned[:, u, :], words[:, u:I // 2:2], ident[:])
+            grouped = keep.tile([P, P * PACK], BF16, name=name + "_grouped", align_bytes=64)
+            nc.scalar.copy(grouped[:].bitcast(F32).rearrange("p (r u) -> p r u", u=2),
+                           turned[:].rearrange("p u r -> p r u"))
+            return quantize(grouped, name)
+
+        kwg = gather(kw, U16, "kwg")
+        ksg = gather(ks, U8, "ksg")
+        q2q = quantize(interleave(q2_raw, "q2_bf"), "q2")
+        qq = quantize(interleave(q_raw, "q_bf"), "q")
+        b_ps = scores(q2q, kwg, ksg, "b_ps")
+        a_ps = scores(qq, kwg, ksg, "a_ps")
+        gt = keep.tile([P, I], F32, name="gt")
+        nc.scalar.activation(gt[:], b_ps[:], ACT.Sigmoid)
+        vwg = gather(vw, U16, "vwg")
+        nmax = keep.tile([P, 1], F32, name="nmax")
+        nc.vector.tensor_reduce(nmax[:], a_ps[:], AXIS.X, ALU.max, negate=True)
+        r = keep.tile([P, I], F32, name="r")
+        nc.scalar.activation(r[:], a_ps[:], ACT.Exp, bias=nmax[:])
+        vsg = gather(vs, U8, "vsg")
+        gq = quantize(interleave(g_raw, "g_bf"), "g")
+        c_ps = scores(gq, vwg, vsg, "c_ps")
+        size_ps = spread(size_col, "size_ps")
+        fs_ps = spread(fs_col, "fs_ps")
+        size_sb = keep.tile([P, I], F32, name="size_sb")
+        nc.scalar.copy(size_sb[:].rearrange("p (n t) -> p n t", t=PACK), size_ps[:].rearrange("p t n -> p n t"))
+
+        w = keep.tile([P, I], F32, name="w")
+        nc.vector.scalar_tensor_tensor(w[:].rearrange("p (n t) -> p n t", t=PACK),
+                                       gt[:].rearrange("p (n t) -> p n t", t=PACK), 1.0,
+                                       fs_ps[:].rearrange("p t n -> p n t"), ALU.subtract, ALU.mult)
+        u = keep.tile([P, I], F32, name="u")
+        nc.vector.scalar_tensor_tensor(u[:], c_ps[:], -1.0, size_sb[:], ALU.mult, ALU.mult)
+        p = keep.tile([P, I], F32, name="p")
+        nz = keep.tile([P, 1], F32, name="nz")
+        nc.vector.scalar_tensor_tensor(p[:], r[:], 1.0, gt[:], ALU.mult, ALU.mult, accum_out=nz[:])
+        up = keep.tile([P, I], F32, name="up")
+        ns = keep.tile([P, 1], F32, name="ns")
+        nc.vector.scalar_tensor_tensor(up[:], u[:], 1.0, p[:], ALU.mult, ALU.mult, accum_out=ns[:])
+        nrz = keep.tile([P, 1], F32, name="nrz")
+        nc.vector.reciprocal(nrz[:], nz[:])
+        mean = keep.tile([P, 1], F32, name="mean")
+        nc.vector.tensor_tensor(mean[:], ns[:], nrz[:], ALU.mult)
+        w2 = keep.tile([P, I], F32, name="w2")
+        nc.vector.scalar_tensor_tensor(w2[:], p[:], nrz[:], w[:], ALU.mult, ALU.mult)
+        gs = keep.tile([P, I], BF16, name="gs", align_bytes=64)
+        nc.vector.scalar_tensor_tensor(gs[:], u[:], mean[:], w2[:], ALU.subtract, ALU.mult)
+        gsq = turn_and_quantize(gs, "gs", "size_ps")
+
+        for j in range(4):
+            ktg = gather(kr[j], BF16, "ktg%d" % j)
+            ktq = turn_and_quantize(ktg, "kt%d" % j, "kt_ps%d" % (j % 2))
+            acc = psum.tile([P, P], F32, name="acc%d" % j, tag=("a_ps", "b_ps", "c_ps", "fs_ps")[j])
+            nc.tensor.matmul_mx(out=acc[:], lhsT=gsq[0][:].bitcast(FP8X4), lhsT_scale=gsq[1][:],
+                                rhs=ktq[0][:].bitcast(FP8X4), rhs_scale=ktq[1][:], start=True, stop=True)
+            y = keep.tile([P, P], F32, name="y%d" % j)
+            nc.vector.tensor_tensor(y[:], acc[:], res_sb[:, j * P:(j + 1) * P], ALU.add)
+            nc.sync.dma_start(out[:, j * P:(j + 1) * P], y[:])

@@ -32,22 +32,18 @@ def tile_attend_bgatedexp_b_q_kernel(tc, query, query2, keys_words, keys_scales,
         offsets = keep.tile([P, I // 16], U16, name="offsets")
         nc.sync.dma_start(offsets[:], offs)
 
-        warm = keep.tile([P, 1], F32, name="warm")
-        warm2 = keep.tile([P, 1], F32, name="warm2")
-        nc.gpsimd.memset(warm[:], 0.0)
-        nc.scalar.activation(warm2[:], warm[:], ACT.Sigmoid)
 
         def load_words(words, name):
             pool_words = keep.tile([P, T], U16, name=name, align_bytes=64)
             nc.sync.dma_start(pool_words[:].bitcast(I32), words[0].bitcast(I32))
             return pool_words
 
-        def load_scales(scales, name):
+        def load_scales(scales, name, zero):
             pool_scales = keep.tile([P, T], U8, name=name, align_bytes=64)
-            nc.vector.memset(pool_scales[:].bitcast(I32), 0)
+            zero.memset(pool_scales[:].bitcast(I32), 0)
             for quad in range(4):
                 nc.sync.dma_start(pool_scales[32 * quad:32 * quad + 4, :].bitcast(I32),
-                                  scales[0, 4 * quad:4 * quad + 4, :].bitcast(I32))
+                              scales[0, 4 * quad:4 * quad + 4, :].bitcast(I32))
             return pool_scales
 
         def load_rows(rows, name):
@@ -60,34 +56,38 @@ def tile_attend_bgatedexp_b_q_kernel(tc, query, query2, keys_words, keys_scales,
             nc.sync.dma_start(col[:], vec.rearrange("o (p t) -> (o p) t", t=PACK))
             return col
 
+        fs_col = load_slot(fs, "fs_col")
+        ks = load_scales(keys_scales, "ks", nc.gpsimd)
         kw = load_words(keys_words, "kw")
-        ks = load_scales(keys_scales, "ks")
         q2_raw = load_rows(query2, "q2_raw")
         q_raw = load_rows(query, "q_raw")
         vw = load_words(vals_words, "vw")
-        vs = load_scales(vals_scales, "vs")
         g_raw = load_rows(gout, "g_raw")
         size_col = load_slot(size, "size_col")
-        fs_col = load_slot(fs, "fs_col")
-        kr = []
-        for j in range(4):
-            rows = keep.tile([P, T], F32, name="kr%d" % j)
-            nc.sync.dma_start(rows[:], keyrows[j * P:(j + 1) * P, :])
-            kr.append(rows)
+        vs = load_scales(vals_scales, "vs", nc.vector)
+        kr = {}
+        for j in (1, 0, 2, 3):
+            kr[j] = keep.tile([P, T], F32, name="kr%d" % j, align_bytes=64)
+            nc.sync.dma_start(kr[j][:], keyrows[j * P:(j + 1) * P, :])
         res_sb = keep.tile([P, D], F32, name="res_sb")
         nc.sync.dma_start(res_sb[:], res)
 
+        warm = keep.tile([P, 1], F32, name="warm")
+        warm2 = keep.tile([P, 1], F32, name="warm2")
+        nc.vector.memset(warm[:], 0.0)
+        nc.scalar.activation(warm2[:], warm[:], ACT.Sigmoid)
         ident = keep.tile([P, P], F32, name="ident")
         make_identity(nc, ident[:])
 
-        def gather(window, dtype, name):
-            got = keep.tile([P, I], dtype, name=name, align_bytes=64)
+        def gather(window, dtype, name, tag):
+            got = keep.tile([P, I], dtype, name=name, tag=tag, align_bytes=64)
             nc.vector.tensor_copy(got[:], window[:].indirect(offsets[:]))
             return got
 
-        def quantize(grouped, name):
-            codes = keep.tile([P, P], U32, name=name + "_codes", align_bytes=64)
-            scales = keep.tile([P, P], U8, name=name + "_scales", align_bytes=64)
+        def quantize(grouped, name, tag):
+            width = grouped.shape[1] // PACK
+            codes = keep.tile([P, width], U32, name=name + "_codes", tag=tag, align_bytes=64)
+            scales = keep.tile([P, width], U8, name=name + "_scales", align_bytes=64)
             nc.vector.quantize_mx(out=codes[:].bitcast(FP8X4), scales=scales[:], in_=grouped[:])
             return codes, scales
 
@@ -109,65 +109,84 @@ def tile_attend_bgatedexp_b_q_kernel(tc, query, query2, keys_words, keys_scales,
                 nc.tensor.transpose(acc[:, t, :], col[:, t:t + 1].to_broadcast([P, P]), ident[:])
             return acc
 
-        def turn_and_quantize(rows_bf, name, tag):
+        def turn(rows_bf, grouped, name, tag):
             words = rows_bf[:].bitcast(F32)
-            turned = psum.tile([P, 2, P], F32, name=name + "_ps", tag=tag)
-            for u in range(2):
-                nc.tensor.transpose(turned[:, u, :], words[:, u:I // 2:2], ident[:])
-            grouped = keep.tile([P, P * PACK], BF16, name=name + "_grouped", align_bytes=64)
-            nc.scalar.copy(grouped[:].bitcast(F32).rearrange("p (r u) -> p r u", u=2),
+            turned = psum.tile([P, 2, P], F32, name=name, tag=tag)
+            for half in range(2):
+                nc.tensor.transpose(turned[:, half, :], words[:, half:I // 2:2], ident[:])
+            nc.scalar.copy(grouped.bitcast(F32).rearrange("p (r u) -> p r u", u=2),
                            turned[:].rearrange("p u r -> p r u"))
-            return quantize(grouped, name)
 
-        kwg = gather(kw, U16, "kwg")
-        ksg = gather(ks, U8, "ksg")
-        q2q = quantize(interleave(q2_raw, "q2_bf"), "q2")
-        qq = quantize(interleave(q_raw, "q_bf"), "q")
+        fs_ps = spread(fs_col, "fs_ps")
+        ksg = gather(ks, U8, "ksg", "ksg")
+        kwg = gather(kw, U16, "kwg", "kwg")
+        q2q = quantize(interleave(q2_raw, "q2_bf"), "q2", "q2c")
+        qq = quantize(interleave(q_raw, "q_bf"), "q", "qc")
         b_ps = scores(q2q, kwg, ksg, "b_ps")
         a_ps = scores(qq, kwg, ksg, "a_ps")
         gt = keep.tile([P, I], F32, name="gt")
         nc.scalar.activation(gt[:], b_ps[:], ACT.Sigmoid)
-        vwg = gather(vw, U16, "vwg")
-        nmax = keep.tile([P, 1], F32, name="nmax")
+        vwg = gather(vw, U16, "vwg", "vwg")
+        nmax = keep.tile([P, 1], F32, name="nmax", tag="vw", align_bytes=64)
         nc.vector.tensor_reduce(nmax[:], a_ps[:], AXIS.X, ALU.max, negate=True)
+        gq = quantize(interleave(g_raw, "g_bf"), "g", "gc")
         r = keep.tile([P, I], F32, name="r")
         nc.scalar.activation(r[:], a_ps[:], ACT.Exp, bias=nmax[:])
-        vsg = gather(vs, U8, "vsg")
-        gq = quantize(interleave(g_raw, "g_bf"), "g")
-        c_ps = scores(gq, vwg, vsg, "c_ps")
         size_ps = spread(size_col, "size_ps")
-        fs_ps = spread(fs_col, "fs_ps")
         size_sb = keep.tile([P, I], F32, name="size_sb")
         nc.scalar.copy(size_sb[:].rearrange("p (n t) -> p n t", t=PACK), size_ps[:].rearrange("p t n -> p n t"))
+        vsg = gather(vs, U8, "vsg", "vsg")
+        c_ps = scores(gq, vwg, vsg, "c_ps")
 
         w = keep.tile([P, I], F32, name="w")
         nc.vector.scalar_tensor_tensor(w[:].rearrange("p (n t) -> p n t", t=PACK),
                                        gt[:].rearrange("p (n t) -> p n t", t=PACK), 1.0,
                                        fs_ps[:].rearrange("p t n -> p n t"), ALU.subtract, ALU.mult)
+        p = keep.tile([P, I], F32, name="p", tag="vs", align_bytes=64)
+        z = keep.tile([P, 1], F32, name="z")
+        nc.vector.scalar_tensor_tensor(p[:], r[:], 1.0, gt[:], ALU.mult, ALU.mult, accum_out=z[:])
         u = keep.tile([P, I], F32, name="u")
         nc.vector.scalar_tensor_tensor(u[:], c_ps[:], -1.0, size_sb[:], ALU.mult, ALU.mult)
-        p = keep.tile([P, I], F32, name="p")
-        nz = keep.tile([P, 1], F32, name="nz")
-        nc.vector.scalar_tensor_tensor(p[:], r[:], 1.0, gt[:], ALU.mult, ALU.mult, accum_out=nz[:])
+        rz = keep.tile([P, 1], F32, name="rz")
+        nc.vector.reciprocal(rz[:], z[:])
         up = keep.tile([P, I], F32, name="up")
-        ns = keep.tile([P, 1], F32, name="ns")
-        nc.vector.scalar_tensor_tensor(up[:], u[:], 1.0, p[:], ALU.mult, ALU.mult, accum_out=ns[:])
-        nrz = keep.tile([P, 1], F32, name="nrz")
-        nc.vector.reciprocal(nrz[:], nz[:])
         mean = keep.tile([P, 1], F32, name="mean")
-        nc.vector.tensor_tensor(mean[:], ns[:], nrz[:], ALU.mult)
-        w2 = keep.tile([P, I], F32, name="w2")
-        nc.vector.scalar_tensor_tensor(w2[:], p[:], nrz[:], w[:], ALU.mult, ALU.mult)
+        nc.vector.scalar_tensor_tensor(up[:], u[:], rz[:], p[:], ALU.mult, ALU.mult, accum_out=mean[:])
+        w2 = keep.tile([P, I], F32, name="w2", align_bytes=64)
+        nc.vector.scalar_tensor_tensor(w2[:], p[:], rz[:], w[:], ALU.mult, ALU.mult)
         gs = keep.tile([P, I], BF16, name="gs", align_bytes=64)
         nc.vector.scalar_tensor_tensor(gs[:], u[:], mean[:], w2[:], ALU.subtract, ALU.mult)
-        gsq = turn_and_quantize(gs, "gs", "size_ps")
 
-        for j in range(4):
-            ktg = gather(kr[j], BF16, "ktg%d" % j)
-            ktq = turn_and_quantize(ktg, "kt%d" % j, "kt_ps%d" % (j % 2))
-            acc = psum.tile([P, P], F32, name="acc%d" % j, tag=("a_ps", "b_ps", "c_ps", "fs_ps")[j])
-            nc.tensor.matmul_mx(out=acc[:], lhsT=gsq[0][:].bitcast(FP8X4), lhsT_scale=gsq[1][:],
-                                rhs=ktq[0][:].bitcast(FP8X4), rhs_scale=ktq[1][:], start=True, stop=True)
-            y = keep.tile([P, P], F32, name="y%d" % j)
-            nc.vector.tensor_tensor(y[:], acc[:], res_sb[:, j * P:(j + 1) * P], ALU.add)
-            nc.sync.dma_start(out[:, j * P:(j + 1) * P], y[:])
+
+        kr_bf = keep.tile([P, T], BF16, name="kr_bf", tag="vw", align_bytes=64)
+        for c in range(4):
+            nc.scalar.activation(kr_bf[:, c * 512:(c + 1) * 512], kr[1][:, c * 512:(c + 1) * 512], ACT.Copy)
+        kt1 = keep.tile([P, I], BF16, name="kt1", align_bytes=64)
+        nc.scalar.activation(kt1[:], kr_bf[:].indirect(offsets[:]), ACT.Copy)
+        first = keep.tile([P, 2 * I], BF16, name="first", tag="vw", align_bytes=64)
+        middle = keep.tile([P, 2 * I], BF16, name="middle", align_bytes=64)
+        turn(gs, first[:, :I], "gs_ps", "size_ps")
+        turn(kt1, middle[:, :I], "kt1_ps", "kt1_ps")
+        kt0 = gather(kr[0], BF16, "kt0", "kt0")
+        turn(kt0, first[:, I:], "kt0_ps", "kt0_ps")
+        kt2 = gather(kr[2], BF16, "kt2", "kt2")
+        first_q = quantize(first, "first", "kr2")
+        turn(kt2, middle[:, I:], "kt2_ps", "kt1_ps")
+        kt3 = gather(kr[3], BF16, "kt3", "kt3")
+
+        last = keep.tile([P, I], BF16, name="last", align_bytes=64)
+        turn(kt3, last[:], "kt3_ps", "b_ps")
+        middle_q = quantize(middle, "middle", "kr3")
+        last_q = quantize(last, "last", "lastc")
+
+        def finish(codes, scales, lo, hi, tag):
+            acc = psum.tile([P, hi - lo], F32, name="acc%d" % lo, tag=tag)
+            nc.tensor.matmul_mx(out=acc[:], lhsT=first_q[0][:, :P].bitcast(FP8X4), lhsT_scale=first_q[1][:, :P],
+                                rhs=codes.bitcast(FP8X4), rhs_scale=scales, start=True, stop=True)
+            y = keep.tile([P, hi - lo], F32, name="y%d" % lo)
+            nc.vector.tensor_tensor(y[:], acc[:], res_sb[:, lo:hi], ALU.add)
+            nc.sync.dma_start(out[:, lo:hi], y[:])
+
+        finish(first_q[0][:, P:], first_q[1][:, P:], 0, P, "a_ps")
+        finish(middle_q[0][:], middle_q[1][:], P, 3 * P, "c_ps")
+        finish(last_q[0][:], last_q[1][:], 3 * P, D, "fs_ps")

@@ -38,16 +38,18 @@ def tile_attend_bgatedexp_b_q_kernel(tc, query, query2, keys_words, keys_scales,
             nc.sync.dma_start(pool_words[:].bitcast(I32), words[0].bitcast(I32))
             return pool_words
 
-        def load_scales(scales, name, zero):
+        def zeroed_scales(name, zero):
             pool_scales = keep.tile([P, T], U8, name=name, align_bytes=64)
             zero.memset(pool_scales[:].bitcast(I32), 0)
-            for quad in range(4):
-                nc.sync.dma_start(pool_scales[32 * quad:32 * quad + 4, :].bitcast(I32),
-                              scales[0, 4 * quad:4 * quad + 4, :].bitcast(I32))
             return pool_scales
 
+        def load_scales(pool_scales, scales, quads):
+            for quad in quads:
+                nc.sync.dma_start(pool_scales[32 * quad:32 * quad + 4, :].bitcast(I32),
+                                  scales[0, 4 * quad:4 * quad + 4, :].bitcast(I32))
+
         def load_rows(rows, name):
-            raw = keep.tile([P, PACK, Q], F32, name=name)
+            raw = keep.tile([P, PACK, Q], F32, name=name, align_bytes=64)
             nc.sync.dma_start(raw[:], rows.rearrange("(p j) w -> p j w", j=PACK))
             return raw
 
@@ -56,19 +58,22 @@ def tile_attend_bgatedexp_b_q_kernel(tc, query, query2, keys_words, keys_scales,
             nc.sync.dma_start(col[:], vec.rearrange("o (p t) -> (o p) t", t=PACK))
             return col
 
-        fs_col = load_slot(fs, "fs_col")
-        ks = load_scales(keys_scales, "ks", nc.gpsimd)
-        kw = load_words(keys_words, "kw")
         q2_raw = load_rows(query2, "q2_raw")
+        ks = zeroed_scales("ks", nc.gpsimd)
+        load_scales(ks, keys_scales, range(4))
+        kw = load_words(keys_words, "kw")
         q_raw = load_rows(query, "q_raw")
         vw = load_words(vals_words, "vw")
-        g_raw = load_rows(gout, "g_raw")
+        fs_col = load_slot(fs, "fs_col")
+        vs = zeroed_scales("vs", nc.vector)
+        load_scales(vs, vals_scales, range(4))
         size_col = load_slot(size, "size_col")
-        vs = load_scales(vals_scales, "vs", nc.vector)
         kr = {}
         for j in (1, 0, 2, 3):
             kr[j] = keep.tile([P, T], F32, name="kr%d" % j, align_bytes=64)
             nc.sync.dma_start(kr[j][:], keyrows[j * P:(j + 1) * P, :])
+            if j == 1:
+                g_raw = load_rows(gout, "g_raw")
         res_sb = keep.tile([P, D], F32, name="res_sb")
         nc.sync.dma_start(res_sb[:], res)
 
@@ -91,15 +96,13 @@ def tile_attend_bgatedexp_b_q_kernel(tc, query, query2, keys_words, keys_scales,
             nc.vector.quantize_mx(out=codes[:].bitcast(FP8X4), scales=scales[:], in_=grouped[:])
             return codes, scales
 
-        def interleave(raw, name):
-            grouped = keep.tile([P, Q * PACK], BF16, name=name, align_bytes=64)
-            nc.scalar.copy(grouped[:].rearrange("p (c i t) -> p c t i", i=4, t=PACK),
+        def interleave(raw, grouped):
+            nc.scalar.copy(grouped.rearrange("p (c i t) -> p c t i", i=4, t=PACK),
                            raw[:].rearrange("p t (c i) -> p c t i", i=4))
-            return grouped
 
-        def scores(lhs, words, scales, name):
+        def scores(lhs, cols, words, scales, name):
             acc = psum.tile([P, I], F32, name=name)
-            nc.tensor.matmul_mx(out=acc[:], lhsT=lhs[0][:].bitcast(FP8X4), lhsT_scale=lhs[1][:],
+            nc.tensor.matmul_mx(out=acc[:], lhsT=lhs[0][:, cols].bitcast(FP8X4), lhsT_scale=lhs[1][:, cols],
                                 rhs=words[:].bitcast(FP4X4), rhs_scale=scales[:], start=True, stop=True)
             return acc
 
@@ -117,76 +120,84 @@ def tile_attend_bgatedexp_b_q_kernel(tc, query, query2, keys_words, keys_scales,
             nc.scalar.copy(grouped.bitcast(F32).rearrange("p (r u) -> p r u", u=2),
                            turned[:].rearrange("p u r -> p r u"))
 
-        fs_ps = spread(fs_col, "fs_ps")
         ksg = gather(ks, U8, "ksg", "ksg")
         kwg = gather(kw, U16, "kwg", "kwg")
-        q2q = quantize(interleave(q2_raw, "q2_bf"), "q2", "q2c")
-        qq = quantize(interleave(q_raw, "q_bf"), "q", "qc")
-        b_ps = scores(q2q, kwg, ksg, "b_ps")
-        a_ps = scores(qq, kwg, ksg, "a_ps")
+        q_bf = keep.tile([P, 2 * Q * PACK], BF16, name="q_bf", align_bytes=64)
+        interleave(q2_raw, q_bf[:, :Q * PACK])
+        interleave(q_raw, q_bf[:, Q * PACK:])
+        qq = quantize(q_bf, "q", "qc")
+        b_ps = scores(qq, slice(0, Q), kwg, ksg, "b_ps")
+        a_ps = scores(qq, slice(Q, 2 * Q), kwg, ksg, "a_ps")
         gt = keep.tile([P, I], F32, name="gt")
         nc.scalar.activation(gt[:], b_ps[:], ACT.Sigmoid)
         vwg = gather(vw, U16, "vwg", "vwg")
-        nmax = keep.tile([P, 1], F32, name="nmax", tag="vw", align_bytes=64)
+        nmax = keep.tile([P, 1], F32, name="nmax", tag="late", align_bytes=64)
         nc.vector.tensor_reduce(nmax[:], a_ps[:], AXIS.X, ALU.max, negate=True)
-        gq = quantize(interleave(g_raw, "g_bf"), "g", "gc")
         r = keep.tile([P, I], F32, name="r")
         nc.scalar.activation(r[:], a_ps[:], ACT.Exp, bias=nmax[:])
-        size_ps = spread(size_col, "size_ps")
-        size_sb = keep.tile([P, I], F32, name="size_sb")
-        nc.scalar.copy(size_sb[:].rearrange("p (n t) -> p n t", t=PACK), size_ps[:].rearrange("p t n -> p n t"))
-        vsg = gather(vs, U8, "vsg", "vsg")
-        c_ps = scores(gq, vwg, vsg, "c_ps")
-
+        fs_ps = spread(fs_col, "fs_ps")
         w = keep.tile([P, I], F32, name="w")
         nc.vector.scalar_tensor_tensor(w[:].rearrange("p (n t) -> p n t", t=PACK),
                                        gt[:].rearrange("p (n t) -> p n t", t=PACK), 1.0,
                                        fs_ps[:].rearrange("p t n -> p n t"), ALU.subtract, ALU.mult)
-        p = keep.tile([P, I], F32, name="p", tag="vs", align_bytes=64)
+        vsg = gather(vs, U8, "vsg", "vsg")
+        p = keep.tile([P, I], F32, name="p", align_bytes=64)
         z = keep.tile([P, 1], F32, name="z")
         nc.vector.scalar_tensor_tensor(p[:], r[:], 1.0, gt[:], ALU.mult, ALU.mult, accum_out=z[:])
-        u = keep.tile([P, I], F32, name="u")
-        nc.vector.scalar_tensor_tensor(u[:], c_ps[:], -1.0, size_sb[:], ALU.mult, ALU.mult)
+        g_bf = keep.tile([P, Q * PACK], BF16, name="g_bf", align_bytes=64)
+        interleave(g_raw, g_bf[:])
+        gq = quantize(g_bf, "g", "gc")
+        size_ps = spread(size_col, "size_ps")
+        c_ps = scores(gq, slice(0, Q), vwg, vsg, "c_ps")
+        rz_s = keep.tile([P, 1], F32, name="rz_s", tag="late", align_bytes=64)
+        nc.vector.reciprocal(rz_s[:], z[:])
+        size_z = keep.tile([P, I], F32, name="size_z", tag="g_raw", align_bytes=64)
+        nc.scalar.activation(size_z[:].rearrange("p (n t) -> p n t", t=PACK), size_ps[:].rearrange("p t n -> p n t"),
+                             ACT.Copy, scale=rz_s[:])
         rz = keep.tile([P, 1], F32, name="rz")
         nc.vector.reciprocal(rz[:], z[:])
+        pw = keep.tile([P, I], F32, name="pw", tag="g_bf", align_bytes=64)
+        nc.vector.tensor_tensor(pw[:], p[:], w[:], ALU.mult)
+        u = keep.tile([P, I], F32, name="u")
+        nc.vector.scalar_tensor_tensor(u[:], c_ps[:], -1.0, size_z[:], ALU.mult, ALU.mult)
         up = keep.tile([P, I], F32, name="up")
         mean = keep.tile([P, 1], F32, name="mean")
         nc.vector.scalar_tensor_tensor(up[:], u[:], rz[:], p[:], ALU.mult, ALU.mult, accum_out=mean[:])
-        w2 = keep.tile([P, I], F32, name="w2", align_bytes=64)
-        nc.vector.scalar_tensor_tensor(w2[:], p[:], rz[:], w[:], ALU.mult, ALU.mult)
         gs = keep.tile([P, I], BF16, name="gs", align_bytes=64)
-        nc.vector.scalar_tensor_tensor(gs[:], u[:], mean[:], w2[:], ALU.subtract, ALU.mult)
+        nc.vector.scalar_tensor_tensor(gs[:], u[:], mean[:], pw[:], ALU.subtract, ALU.mult)
 
 
-        kr_bf = keep.tile([P, T], BF16, name="kr_bf", tag="vw", align_bytes=64)
-        for c in range(4):
-            nc.scalar.activation(kr_bf[:, c * 512:(c + 1) * 512], kr[1][:, c * 512:(c + 1) * 512], ACT.Copy)
+        kr_bf = keep.tile([P, T], BF16, name="kr_bf", tag="late", align_bytes=64)
+        nc.scalar.activation(kr_bf[:], kr[1][:], ACT.Copy)
         kt1 = keep.tile([P, I], BF16, name="kt1", align_bytes=64)
         nc.scalar.activation(kt1[:], kr_bf[:].indirect(offsets[:]), ACT.Copy)
-        first = keep.tile([P, 2 * I], BF16, name="first", tag="vw", align_bytes=64)
-        middle = keep.tile([P, 2 * I], BF16, name="middle", align_bytes=64)
-        turn(gs, first[:, :I], "gs_ps", "size_ps")
-        turn(kt1, middle[:, :I], "kt1_ps", "kt1_ps")
-        kt0 = gather(kr[0], BF16, "kt0", "kt0")
-        turn(kt0, first[:, I:], "kt0_ps", "kt0_ps")
-        kt2 = gather(kr[2], BF16, "kt2", "kt2")
-        first_q = quantize(first, "first", "kr2")
-        turn(kt2, middle[:, I:], "kt2_ps", "kt1_ps")
+        early = keep.tile([P, 4 * I], BF16, name="early", tag="late", align_bytes=64)
+        kt0 = gather(kr[0], BF16, "kt0", "g_raw")
+        turn(kt1, early[:, 2 * I:3 * I], "kt1_ps", "kt1_ps")
+        turn(kt0, early[:, I:2 * I], "kt0_ps", "kt0_ps")
+        turn(gs, early[:, :I], "gs_ps", "size_ps")
+        kt2 = gather(kr[2], BF16, "kt2", "p")
+        turn(kt2, early[:, 3 * I:], "kt2_ps", "kt1_ps")
         kt3 = gather(kr[3], BF16, "kt3", "kt3")
 
         last = keep.tile([P, I], BF16, name="last", align_bytes=64)
         turn(kt3, last[:], "kt3_ps", "b_ps")
-        middle_q = quantize(middle, "middle", "kr3")
+        early_q = quantize(early, "early", "kr3")
         last_q = quantize(last, "last", "lastc")
 
-        def finish(codes, scales, lo, hi, tag):
-            acc = psum.tile([P, hi - lo], F32, name="acc%d" % lo, tag=tag)
-            nc.tensor.matmul_mx(out=acc[:], lhsT=first_q[0][:, :P].bitcast(FP8X4), lhsT_scale=first_q[1][:, :P],
+        def product(acc, codes, scales):
+            nc.tensor.matmul_mx(out=acc, lhsT=early_q[0][:, :P].bitcast(FP8X4), lhsT_scale=early_q[1][:, :P],
                                 rhs=codes.bitcast(FP8X4), rhs_scale=scales, start=True, stop=True)
-            y = keep.tile([P, hi - lo], F32, name="y%d" % lo)
+
+        def finish(acc, lo, hi, tag):
+            y = keep.tile([P, hi - lo], F32, name="y%d" % lo, tag=tag, align_bytes=64)
             nc.vector.tensor_tensor(y[:], acc[:], res_sb[:, lo:hi], ALU.add)
             nc.sync.dma_start(out[:, lo:hi], y[:])
 
-        finish(first_q[0][:, P:], first_q[1][:, P:], 0, P, "a_ps")
-        finish(middle_q[0][:], middle_q[1][:], P, 3 * P, "c_ps")
-        finish(last_q[0][:], last_q[1][:], 3 * P, D, "fs_ps")
+        acc = psum.tile([P, 3 * P], F32, name="acc", tag="a_ps")
+        product(acc[:, :2 * P], early_q[0][:, P:3 * P], early_q[1][:, P:3 * P])
+        product(acc[:, 2 * P:], early_q[0][:, 3 * P:], early_q[1][:, 3 * P:])
+        acc3 = psum.tile([P, P], F32, name="acc3", tag="c_ps")
+        product(acc3[:], last_q[0][:], last_q[1][:])
+        finish(acc, 0, 3 * P, "last")
+        finish(acc3, 3 * P, D, "y3")

@@ -45,8 +45,8 @@ def tile_attend_bgatedexp_b_q_kernel(tc, query, query2, keys_words, keys_scales,
 
         def load_scales(pool_scales, scales, quads):
             for quad in quads:
-                nc.sync.dma_start(pool_scales[32 * quad:32 * quad + 4, :].bitcast(I32),
-                                  scales[0, 4 * quad:4 * quad + 4, :].bitcast(I32))
+                nc.sync.dma_start(pool_scales[quad:P:32, :].bitcast(I32),
+                                  scales[0, quad:16:4, :].bitcast(I32))
 
         def load_rows(rows, name):
             raw = keep.tile([P, PACK, Q], F32, name=name, align_bytes=64)

from contextlib import ExitStack

import concourse.mybir as mybir
from concourse.masks import make_identity

D, E, T, I, Q = 512, 512, 2048, 512, 128
FLOPS = 2 * Q * I * (2 * D + E) + 2 * I * Q * D

F32 = mybir.dt.float32
BF16 = mybir.dt.bfloat16
I32 = mybir.dt.int32
U32 = mybir.dt.uint32
U16 = mybir.dt.uint16
U8 = mybir.dt.uint8
FP8X4 = mybir.dt.float8_e4m3fn_x4
FP4X4 = mybir.dt.float4_e2m1fn_x4
ACT = mybir.ActivationFunctionType
ALU = mybir.AluOpType
AXIS = mybir.AxisListType

P = 128
PACK = 4


def tile_attend_bgatedexp_b_q_kernel(tc, query, query2, keys_words, keys_scales, gout, vals_words, vals_scales,
                                      size, fs, keyrows, res, offs, out):
    nc = tc.nc
    with ExitStack() as ctx:
        keep = ctx.enter_context(tc.tile_pool(name="keep", bufs=1))
        psum = ctx.enter_context(tc.psum_pool(name="psum", bufs=1))

        offsets = keep.tile([P, I // 16], U16, name="offsets")
        nc.sync.dma_start(offsets[:], offs)


        def load_words(words, name):
            pool_words = keep.tile([P, T], U16, name=name, align_bytes=64)
            nc.sync.dma_start(pool_words[:].bitcast(I32), words[0].bitcast(I32))
            return pool_words

        def zeroed_scales(name, zero):
            pool_scales = keep.tile([P, T], U8, name=name, align_bytes=64)
            zero.memset(pool_scales[:].bitcast(I32), 0)
            return pool_scales

        def load_scales(pool_scales, scales, quads):
            for quad in quads:
                nc.sync.dma_start(pool_scales[quad:P:32, :].bitcast(I32),
                                  scales[0, quad:16:4, :].bitcast(I32))

        def load_rows(rows, name):
            raw = keep.tile([P, PACK, Q], F32, name=name, align_bytes=64)
            nc.sync.dma_start(raw[:], rows.rearrange("(p j) w -> p j w", j=PACK))
            return raw

        def load_slot(vec, name):
            col = keep.tile([P, PACK], F32, name=name)
            nc.sync.dma_start(col[:], vec.rearrange("o (p t) -> (o p) t", t=PACK))
            return col

        q2_raw = load_rows(query2, "q2_raw")
        ks = zeroed_scales("ks", nc.gpsimd)
        load_scales(ks, keys_scales, range(4))
        kw = load_words(keys_words, "kw")
        q_raw = load_rows(query, "q_raw")
        vw = load_words(vals_words, "vw")
        fs_col = load_slot(fs, "fs_col")
        vs = zeroed_scales("vs", nc.vector)
        load_scales(vs, vals_scales, range(4))
        size_col = load_slot(size, "size_col")
        kr = {}
        for j in (1, 0, 2, 3):
            kr[j] = keep.tile([P, T], F32, name="kr%d" % j, align_bytes=64)
            nc.sync.dma_start(kr[j][:], keyrows[j * P:(j + 1) * P, :])
            if j == 1:
                g_raw = load_rows(gout, "g_raw")
        res_sb = keep.tile([P, D], F32, name="res_sb")
        nc.sync.dma_start(res_sb[:], res)

        warm = keep.tile([P, 1], F32, name="warm")
        warm2 = keep.tile([P, 1], F32, name="warm2")
        nc.vector.memset(warm[:], 0.0)
        nc.scalar.activation(warm2[:], warm[:], ACT.Sigmoid)
        ident = keep.tile([P, P], F32, name="ident")
        make_identity(nc, ident[:])

        def gather(window, dtype, name, tag):
            got = keep.tile([P, I], dtype, name=name, tag=tag, align_bytes=64)
            nc.vector.tensor_copy(got[:], window[:].indirect(offsets[:]))
            return got

        def quantize(grouped, name, tag):
            width = grouped.shape[1] // PACK
            codes = keep.tile([P, width], U32, name=name + "_codes", tag=tag, align_bytes=64)
            scales = keep.tile([P, width], U8, name=name + "_scales", align_bytes=64)
            nc.vector.quantize_mx(out=codes[:].bitcast(FP8X4), scales=scales[:], in_=grouped[:])
            return codes, scales

        def interleave(raw, grouped):
            nc.scalar.copy(grouped.rearrange("p (c i t) -> p c t i", i=4, t=PACK),
                           raw[:].rearrange("p t (c i) -> p c t i", i=4))

        def scores(lhs, cols, words, scales, name):
            acc = psum.tile([P, I], F32, name=name)
            nc.tensor.matmul_mx(out=acc[:], lhsT=lhs[0][:, cols].bitcast(FP8X4), lhsT_scale=lhs[1][:, cols],
                                rhs=words[:].bitcast(FP4X4), rhs_scale=scales[:], start=True, stop=True)
            return acc

        def spread(col, name):
            acc = psum.tile([P, PACK, P], F32, name=name)
            for t in range(PACK):
                nc.tensor.transpose(acc[:, t, :], col[:, t:t + 1].to_broadcast([P, P]), ident[:])
            return acc

        def turn(rows_bf, grouped, name, tag):
            words = rows_bf[:].bitcast(F32)
            turned = psum.tile([P, 2, P], F32, name=name, tag=tag)
            for half in range(2):
                nc.tensor.transpose(turned[:, half, :], words[:, half:I // 2:2], ident[:])
            nc.scalar.copy(grouped.bitcast(F32).rearrange("p (r u) -> p r u", u=2),
                           turned[:].rearrange("p u r -> p r u"))

        ksg = gather(ks, U8, "ksg", "ksg")
        kwg = gather(kw, U16, "kwg", "kwg")
        q_bf = keep.tile([P, 2 * Q * PACK], BF16, name="q_bf", align_bytes=64)
        interleave(q2_raw, q_bf[:, :Q * PACK])
        interleave(q_raw, q_bf[:, Q * PACK:])
        qq = quantize(q_bf, "q", "qc")
        b_ps = scores(qq, slice(0, Q), kwg, ksg, "b_ps")
        a_ps = scores(qq, slice(Q, 2 * Q), kwg, ksg, "a_ps")
        gt = keep.tile([P, I], F32, name="gt")
        nc.scalar.activation(gt[:], b_ps[:], ACT.Sigmoid)
        vwg = gather(vw, U16, "vwg", "vwg")
        nmax = keep.tile([P, 1], F32, name="nmax", tag="late", align_bytes=64)
        nc.vector.tensor_reduce(nmax[:], a_ps[:], AXIS.X, ALU.max, negate=True)
        r = keep.tile([P, I], F32, name="r")
        nc.scalar.activation(r[:], a_ps[:], ACT.Exp, bias=nmax[:])
        fs_ps = spread(fs_col, "fs_ps")
        w = keep.tile([P, I], F32, name="w")
        nc.vector.scalar_tensor_tensor(w[:].rearrange("p (n t) -> p n t", t=PACK),
                                       gt[:].rearrange("p (n t) -> p n t", t=PACK), 1.0,
                                       fs_ps[:].rearrange("p t n -> p n t"), ALU.subtract, ALU.mult)
        vsg = gather(vs, U8, "vsg", "vsg")
        p = keep.tile([P, I], F32, name="p", align_bytes=64)
        z = keep.tile([P, 1], F32, name="z")
        nc.vector.scalar_tensor_tensor(p[:], r[:], 1.0, gt[:], ALU.mult, ALU.mult, accum_out=z[:])
        g_bf = keep.tile([P, Q * PACK], BF16, name="g_bf", align_bytes=64)
        interleave(g_raw, g_bf[:])
        gq = quantize(g_bf, "g", "gc")
        size_ps = spread(size_col, "size_ps")
        c_ps = scores(gq, slice(0, Q), vwg, vsg, "c_ps")
        rz_s = keep.tile([P, 1], F32, name="rz_s", tag="late", align_bytes=64)
        nc.vector.reciprocal(rz_s[:], z[:])
        size_z = keep.tile([P, I], F32, name="size_z", tag="g_raw", align_bytes=64)
        nc.scalar.activation(size_z[:].rearrange("p (n t) -> p n t", t=PACK), size_ps[:].rearrange("p t n -> p n t"),
                             ACT.Copy, scale=rz_s[:])
        rz = keep.tile([P, 1], F32, name="rz")
        nc.vector.reciprocal(rz[:], z[:])
        pw = keep.tile([P, I], F32, name="pw", tag="g_bf", align_bytes=64)
        nc.vector.tensor_tensor(pw[:], p[:], w[:], ALU.mult)
        u = keep.tile([P, I], F32, name="u")
        nc.vector.scalar_tensor_tensor(u[:], c_ps[:], -1.0, size_z[:], ALU.mult, ALU.mult)
        up = keep.tile([P, I], F32, name="up")
        mean = keep.tile([P, 1], F32, name="mean")
        nc.vector.scalar_tensor_tensor(up[:], u[:], rz[:], p[:], ALU.mult, ALU.mult, accum_out=mean[:])
        gs = keep.tile([P, I], BF16, name="gs", align_bytes=64)
        nc.vector.scalar_tensor_tensor(gs[:], u[:], mean[:], pw[:], ALU.subtract, ALU.mult)


        kr_bf = keep.tile([P, T], BF16, name="kr_bf", tag="late", align_bytes=64)
        nc.scalar.activation(kr_bf[:], kr[1][:], ACT.Copy)
        kt1 = keep.tile([P, I], BF16, name="kt1", align_bytes=64)
        nc.scalar.activation(kt1[:], kr_bf[:].indirect(offsets[:]), ACT.Copy)
        early = keep.tile([P, 4 * I], BF16, name="early", tag="late", align_bytes=64)
        kt0 = gather(kr[0], BF16, "kt0", "g_raw")
        turn(kt1, early[:, 2 * I:3 * I], "kt1_ps", "kt1_ps")
        turn(kt0, early[:, I:2 * I], "kt0_ps", "kt0_ps")
        turn(gs, early[:, :I], "gs_ps", "size_ps")
        kt2 = gather(kr[2], BF16, "kt2", "p")
        turn(kt2, early[:, 3 * I:], "kt2_ps", "kt1_ps")
        kt3 = gather(kr[3], BF16, "kt3", "kt3")

        last = keep.tile([P, I], BF16, name="last", align_bytes=64)
        turn(kt3, last[:], "kt3_ps", "b_ps")
        early_q = quantize(early, "early", "kr3")
        last_q = quantize(last, "last", "lastc")

        def product(acc, codes, scales):
            nc.tensor.matmul_mx(out=acc, lhsT=early_q[0][:, :P].bitcast(FP8X4), lhsT_scale=early_q[1][:, :P],
                                rhs=codes.bitcast(FP8X4), rhs_scale=scales, start=True, stop=True)

        def finish(acc, lo, hi, tag):
            y = keep.tile([P, hi - lo], F32, name="y%d" % lo, tag=tag, align_bytes=64)
            nc.vector.tensor_tensor(y[:], acc[:], res_sb[:, lo:hi], ALU.add)
            nc.sync.dma_start(out[:, lo:hi], y[:])

        acc = psum.tile([P, 3 * P], F32, name="acc", tag="a_ps")
        product(acc[:, :2 * P], early_q[0][:, P:3 * P], early_q[1][:, P:3 * P])
        product(acc[:, 2 * P:], early_q[0][:, 3 * P:], early_q[1][:, 3 * P:])
        acc3 = psum.tile([P, P], F32, name="acc3", tag="c_ps")
        product(acc3[:], last_q[0][:], last_q[1][:])
        finish(acc, 0, 3 * P, "last")
        finish(acc3, 3 * P, D, "y3")
